import numpy as np, ml_dtypes
CORES = [13,21,141,149]
N = 4
import mx_ref
BF = ml_dtypes.bfloat16
def cols(t, e):
    v = np.concatenate([t.reshape(128, -1, 4), np.zeros((128, 1, 4), BF)], axis=1)
    return np.ascontiguousarray(v[:, e]).reshape(128, -1)
def cut(t, i, w=512):
    return t[:, w * i:w * i + w]
def f(rng, *shape):
    return mx_ref.flush((rng.standard_normal(shape, dtype=np.float32) * np.exp2(rng.integers(-2, 3, shape[:-1] + (1,)))).astype(BF))
def wide(rng, *shape, cols=0):
    v = rng.standard_normal(shape, dtype=np.float32) * np.exp2(rng.integers(-12, 13, shape)).astype(np.float32)
    if cols: v *= np.repeat(np.exp2(rng.integers(-cols, cols + 1, shape[:-2] + (1, shape[-1] // 4))) * (rng.random(shape[:-2] + (1, shape[-1] // 4)) > 0.0625), 4, axis=-1).astype(np.float32)
    return mx_ref.flush(v.astype(BF))
T, CAPP = 512, 48
def normal(rng, *shape):
    return mx_ref.flush(rng.standard_normal(shape, dtype=np.float32).astype(BF))
def once(rng, case):
    g = wide if case == "spread" else normal
    c = g(rng, N, 128, 4 * T).transpose(1, 0, 2).reshape(128, N * T, 4)
    v = (wide if case == "spread" else f)(rng, N, 128, 4 * T)
    if case in ("near", "ties"):
        e = np.stack([q * T + rng.permutation(T) for q in range(N)])
        m = T // 16; s = int(rng.integers(1, N))
        sets = [(e[:, :2 * m], np.roll(e[:, 2 * m:4 * m], -s, axis=0)),
                (e[:, 4 * m:7 * m], e[:, 7 * m:10 * m]),
                (e[:, 10 * m:11 * m], e[:, 11 * m:12 * m], e[:, 12 * m:13 * m]),
                (e[:, 13 * m:14 * m], e[:, 14 * m:15 * m], np.roll(e[:, 15 * m:], -s, axis=0))]
        first, at, place = np.zeros(N * T, int), np.zeros(N * T, int), rng.integers(0, 512, N * T)
        for l in sets:
            l = np.sort(np.stack(l), axis=0)
            for i in range(len(l)):
                first[l[i]] = l[0]; at[l[i]] = i; place[l[i]] = place[l[0]]
        c = c[:, first]
        if case == "near": c[place // 4, np.arange(N * T), place % 4] = (1 + 0.25 * at).astype(BF)
    if case == "negative":
        z = normal(rng, 128, 1, 4).astype(np.float32) * np.float32(2.0 ** 20)
        c = mx_ref.flush((c.astype(np.float32) * np.float32(2.0 ** 20) + z).astype(BF))
    an, fb = [], []
    for r in range(N):
        if case == "ties":
            n = rng.permutation([CAPP, CAPP, 128 - 2 * CAPP, 0]); to = []
            for q in range(N):
                w = rng.choice(q * T + np.flatnonzero(at[q * T:q * T + T] < 2), n[q])
                w[:12] = w[:1]; to += list(w)
            to = np.array(to)
        else:
            n = 24 + rng.multinomial(32, np.full(N, np.divide(1, N)))
            while n.max() > 40: n = 24 + rng.multinomial(32, np.full(N, np.divide(1, N)))
            to = np.repeat(np.arange(N) * T, n) + rng.integers(0, T, 128)
        to = rng.permutation(to)
        other = (to + rng.integers(1, N * T, 128)) % (N * T)
        away = (to + rng.integers(1, N * T, 128)) % (N * T)
        h = rng.permutation(128) < (128 if case == "forbid" else 64 if case in ("plain", "spread") else 0)
        best, second = np.where(h, other, to), np.where(h, to, other)
        ban = np.where(h, other, away)
        if case == "ties": ban = np.where(at[to] > 0, first[to], away)
        t = c[:, best].astype(np.float32) + np.float32(0.5) * c[:, second].astype(np.float32)
        if case == "negative": t = t - np.float32(4.5) * z
        if case == "near":
            t[place[to] // 4, np.arange(128), place[to] % 4] = np.where(at[to] > 0, 1, -1) * np.exp2(-rng.integers(1, 6, 128))
        an.append(mx_ref.flush(t.astype(BF)).reshape(128, 512)); fb.append(ban.astype(np.int32).reshape(128, 1))
    k = np.ascontiguousarray(c.reshape(128, N, 4 * T).transpose(1, 0, 2))
    return {"an": np.stack(an), "k": k, "v": v, "u": f(rng, N, 128, 512), "fb": np.stack(fb)}
def planted(d, case):
    if case not in ("near", "negative", "ties"): return True
    s = scores(d["an"], d["k"])
    if case == "negative": return bool((s < 0).all())
    s = allowed(s, d["fb"])
    if case == "near":
        top = np.partition(s, N * T - 2, axis=1)[:, -2:]
        gap = top[:, 1] - top[:, 0]
        return bool(((gap > 0) & (gap < 2.0 ** -9 * np.abs(top[:, 1]))).sum(axis=1).min() >= 20)
    w = np.argmax(s, axis=1)
    per = (s == s.max(axis=1, keepdims=True)).reshape(N, N, T, 128).sum(axis=2)
    within = np.take_along_axis(per, (w // T)[:, None], axis=1)[:, 0] > 1
    across = (per > 0).sum(axis=1) > 1
    return bool(within.sum(axis=1).min() >= 10 and across.sum() >= 20)
def draw(rng, case):
    for _ in range(50):
        d = once(rng, case)
        if not check_inputs(d) and planted(d, case): return d
    raise RuntimeError("no draw in 50 tries: " + case)
def setup_inputs(rng):
    return draw(rng, "plain")
def setup_inputs_forbid(rng):
    return draw(rng, "forbid")
def setup_inputs_near(rng):
    return draw(rng, "near")
def setup_inputs_negative(rng):
    return draw(rng, "negative")
def setup_inputs_spread(rng):
    return draw(rng, "spread")
def setup_inputs_ties(rng):
    return draw(rng, "ties")
def scores(an, k):
    kq = [mx_ref.quantize(cut(k[q], j)) for q in range(N) for j in range(T // 128)]
    out = []
    for r in range(N):
        a = mx_ref.quantize(an[r])
        out.append(np.concatenate([mx_ref.matmul(b, a) for b in kq]))
    return np.stack(out)
def allowed(s, fb):
    for r in range(N): s[r][fb[r][:, 0], np.arange(128)] = -np.inf
    return s
def winners(an, k, fb):
    return np.argmax(allowed(scores(an, k), fb), axis=1)
def check_inputs(d):
    if d["fb"].min() < 0 or d["fb"].max() >= N * T: return ["fb"]
    b = []; w = winners(d["an"], d["k"], d["fb"])
    for r in range(N):
        if np.bincount(w[r] // T, minlength=N).max() > CAPP: b.append("winners")
    return b
def reference(an, k, v, u, fb):
    w = winners(an, k, fb)
    allv = np.concatenate([v[q] for q in range(N)], axis=1)
    y = np.zeros((N, 128, 128), np.float32)
    for r in range(N):
        y[r] = mx_ref.matmul(mx_ref.quantize(u[r]), mx_ref.quantize(cols(allv, w[r])))
    return {"y": y, "win": w.astype(np.float32).reshape(N, 128, 1)}

@@ -1,0 +1,368 @@
+from concourse.bass import DstId, RemoteDMATransfer
+from concourse.mybir import dt, AluOpType, AxisListType, ActivationFunctionType
+
+OP = AluOpType
+ACT = ActivationFunctionType
+C8 = "float8_e4m3fn_x4"
+LOW = -1.0e29
+
+SCRATCH = {
+    "at": ("sbuf", [128, 512], "bfloat16"),
+    "kt": ("sbuf", [128, 2048], "bfloat16"),
+    "vt": ("sbuf", [128, 2048], "bfloat16"),
+    "ut": ("sbuf", [128, 512], "bfloat16"),
+    "fbd": ("dram", [128, 1], "int32"),
+    "fbo": ("sbuf", [128, 1], "int32"),
+    "qa": ("sbuf", [128, 128], C8), "qas": ("sbuf", [128, 128], "uint8"),
+    "qk": ("sbuf", [128, 512], C8), "qks": ("sbuf", [128, 512], "uint8"),
+    "qu": ("sbuf", [128, 128], C8), "qus": ("sbuf", [128, 128], "uint8"),
+    "la": ("sbuf", [128, 512], C8), "las": ("sbuf", [128, 512], "uint8"),
+    "lf": ("sbuf", [128, 4], "int32"),
+    "best": ("sbuf", [128, 16], "float32"),
+    "lz": ("sbuf", [128, 512], C8), "lzs": ("sbuf", [128, 512], "uint8"),
+    "rfb": ("dram", [128, 1], "int32"),
+    "rac": ("sbuf", [128, 128], C8), "ras": ("sbuf", [128, 128], "uint8"),
+    "rbest": ("sbuf", [128, 2], "float32"),
+    "rzc": ("sbuf", [128, 128], C8), "rzs": ("sbuf", [128, 128], "uint8"),
+    "ones": ("sbuf", [128, 512], "float32"),
+    "num": ("sbuf", [128, 512], "float32"),
+    "im": ("sbuf", [128, 64], "int32"), "am": ("sbuf", [128, 64], "int32"),
+    "mask": ("sbuf", [128, 64], "float32"),
+    "keep": ("sbuf", [128, 128], "float32"),
+    "ip": ("sbuf", [128, 4], "int32"), "i1": ("sbuf", [128, 4], "int32"),
+    "i2": ("sbuf", [128, 4], "int32"), "i3": ("sbuf", [128, 4], "int32"),
+    "cp": ("sbuf", [128, 4], "float32"), "cd": ("sbuf", [128, 4], "float32"),
+    "cq": ("sbuf", [128, 4], "float32"), "nq": ("sbuf", [128, 4], "float32"),
+    "mx": ("sbuf", [128, 1], "float32"), "t4": ("sbuf", [128, 4], "float32"),
+    "c1": ("sbuf", [128, 4], "float32"), "c2": ("sbuf", [128, 4], "float32"),
+    "c3": ("sbuf", [128, 4], "float32"),
+    "pick": ("sbuf", [128, 1], "float32"), "won": ("sbuf", [128, 1], "float32"),
+    "xf": ("sbuf", [128, 64], "float32"), "yf": ("sbuf", [128, 64], "float32"),
+    "wf": ("sbuf", [128, 64], "float32"), "of": ("sbuf", [128, 8], "uint16"),
+    "prod": ("sbuf", [128, 512], "float32"),
+    "ysb": ("sbuf", [128, 128], "float32"),
+    "ps": ("psum", [128, 2048], "float32"),
+    "pu": ("psum", [128, 2048], "float32"),
+}
+for _i in range(4):
+    SCRATCH["fn%d" % _i] = ("sbuf", [128, 1], "float32")
+    SCRATCH["pen%d" % _i] = ("sbuf", [128, 512], "float32")
+    SCRATCH["ms%d" % _i] = ("sbuf", [128, 512], "float32")
+    SCRATCH["run%d" % _i] = ("sbuf", [128, 520], "float32")
+    SCRATCH["sink%d" % _i] = ("sbuf", [128, 512], "bfloat16")
+for _j in range(2):
+    SCRATCH["x%d" % _j] = ("sbuf", [128, 128], "float32")
+    SCRATCH["xt%d" % _j] = ("sbuf", [128, 128], "float32")
+    SCRATCH["xw%d" % _j] = ("sbuf", [128, 128], "float32")
+    SCRATCH["off%d" % _j] = ("sbuf", [128, 16], "uint16")
+    SCRATCH["z%d" % _j] = ("sbuf", [128, 1024], "bfloat16")
+    SCRATCH["zq%d" % _j] = ("sbuf", [128, 256], C8)
+    SCRATCH["zqs%d" % _j] = ("sbuf", [128, 256], "uint8")
+
+SEMAPHORES = (
+    ["ld_a", "ld_k", "ld_v", "ld_u", "ld_fd", "ld_fo", "st"]
+    + ["sf", "sx", "sp", "sb", "sz"]
+    + ["rf_in", "rac_in", "ras_in", "rb_in", "rzc_in", "rzs_in", "rsent"]
+    + ["%s%d" % (n, i) for n in ("a_in", "f_in", "b_in", "z_in") for i in range(4)]
+    + ["io", "k1", "k2", "k3", "k4", "k5", "qa_ok", "qk_ok", "qu_ok"]
+    + ["%s%d" % (n, i) for n in ("fn_ok", "pen_ok", "mm_ok", "ms_ok", "run_ok", "idx_ok", "pu_ok") for i in range(4)]
+    + ["%s%d" % (n, j) for n in ("x_ok", "xt_ok", "xw_ok", "o1_ok", "o2_ok", "zv_ok", "zs_ok", "zq_ok") for j in range(2)]
+    + ["m1", "m2", "m3", "m4", "m5", "pick_ok", "won_ok", "xf_ok", "yf_ok", "wf_ok", "of1_ok", "of2_ok", "uv", "us", "y_ok"]
+)
+
+
+def bits(engines):
+    m = 0
+    for e in engines:
+        m |= 1 << e
+    return m
+
+
+def roads(T, topo):
+    relay = {}
+    for r, a in enumerate(T.cores):
+        for d, b in enumerate(T.cores):
+            if d == r or topo.may_write(a, b):
+                continue
+            near = topo.host(a) == topo.host(b)
+            c = [x for x in topo.cores_of(a) if x != a and topo.may_write(x, b) and (topo.die(x) == topo.die(a)) == near]
+            relay[(r, d)] = c[0]
+    return relay
+
+
+def u8(view):
+    return view.bitcast(dt.uint8)
+
+
+def rank_program(g, core, T, topo):
+    relay = roads(T, topo)
+    rank = T.rank_of(core)
+    if rank is None:
+        for (r, d), c in relay.items():
+            if c == core:
+                relay_program(g, core, T, topo, r, d)
+        return
+    S = T.sem
+    V, P, A, Y = g.vector, g.tensor, g.scalar, g.sync
+    direct = [d for d in range(len(T.cores)) if d != rank and (rank, d) not in relay]
+    cross = [d for d in range(len(T.cores)) if (rank, d) in relay]
+    cross.sort(key=lambda d: topo.die(relay[(rank, d)]) != topo.die(core))
+    mate = direct[0]
+    order = [rank, mate] + cross
+    n = {}
+
+    def done(q, name, k=1):
+        q.then_inc(S[name], k)
+        n[name] = n.get(name, 0) + k
+
+    def need(queue, *names):
+        for x in names:
+            queue.wait_ge(S[x], n[x])
+
+    done(Y.dma_start(T.at[:], T.an[:]), "ld_a", 16)
+    done(A.dma_start(T.fbd[:], T.fb[:]), "ld_fd", 16)
+    done(A.dma_start(T.fbo[:], T.fb[:]), "ld_fo", 16)
+    done(Y.dma_start(T.kt[:], T.k[:]), "ld_k", 16)
+
+    done(g.iota(T.im[:], [[-16, 2], [0, 2], [-1, 16]], 64, 1), "io")
+    done(g.iota(T.ip[:], [[0, 4]], 0, 1), "io")
+    done(g.iota(T.cp[:], [[128, 4]], 0, 1, allow_small_or_imprecise_dtypes=True), "io")
+    done(g.iota(T.nq[:], [[512, 4]], 0, 0, allow_small_or_imprecise_dtypes=True), "io")
+    done(V.memset(T.ones[:], 1.0), "k1")
+    done(V.memset(T.keep[:], 1.0), "k1")
+    need(V, "k1")
+    done(V.tensor_tensor_scan(T.num[:], T.ones[:], T.ones[:], -1.0, OP.add, OP.mult), "k2")
+    done(V.memset(T.keep[:, 0:128:32], 0.0), "k2")
+    need(V, "io")
+    done(V.tensor_scalar(T.am[:], T.im[:], 31, None, OP.bitwise_and), "k3")
+    done(V.tensor_scalar(T.i1[:], T.ip[:], 4, 1, OP.arith_shift_right, OP.bitwise_and), "k3")
+    done(V.tensor_scalar(T.i2[:], T.ip[:], 6, None, OP.arith_shift_right), "k3")
+    need(V, "k2", "k3")
+    done(V.tensor_scalar(T.mask[:], T.am[:], 0.0, 4.0, OP.is_equal, OP.mult), "k4")
+    done(V.tensor_tensor(T.i3[:], T.i1[:], T.i2[:], OP.subtract), "k4")
+    need(V, "k4")
+    done(V.tensor_scalar(T.cd[:], T.i3[:], 48.0, None, OP.mult), "k5")
+    need(V, "k5")
+    done(V.tensor_tensor(T.cq[:], T.cp[:], T.cd[:], OP.add), "k5")
+
+    need(V, "ld_a")
+    done(V.quantize_mx(T.qa[:], T.qas[:], T.at[:]), "qa_ok")
+
+    far = topo.engines(core, T.cores[mate])
+    chip = topo.engines(core, relay[(rank, cross[0])])
+    rest = [e for e in chip if e not in far]
+
+    def xfer(dst, mask, sem, src, to):
+        rid, pid = topo.addr(dst, core)
+        return RemoteDMATransfer(dst_ids=[DstId(rid=rid, pnc=pid)], dma_engine_mask=mask, remote_sem=S[sem], src=src, dst=to)
+
+    def fused(sem, *ts):
+        g.remote_dma_fused(list(ts), local_sem=S[sem])
+
+    rl = [relay[(rank, d)] for d in cross]
+    dm = T.cores[mate]
+    half = [bits(chip[1::2]), bits(chip[0::2])]
+    need(g, "ld_fd")
+    fused("sf",
+          xfer(rl[0], bits(rest[0:2]), "rf_in", T.fbd[:], T.rfb[:]),
+          xfer(rl[1], bits(rest[2:4]), "rf_in", T.fbd[:], T.rfb[:]),
+          xfer(dm, bits(far[0::2]), "f_in%d" % rank, T.fbd[:], T.lf[:, rank:rank + 1]))
+    n["sf"] = 2 + 2 + len(far[0::2])
+    need(g, "qa_ok")
+    fused("sx",
+          xfer(rl[0], half[0], "rac_in", u8(T.qa[:]), u8(T.rac[:])),
+          xfer(rl[1], half[1], "rac_in", u8(T.qa[:]), u8(T.rac[:])))
+    fused("sx",
+          xfer(rl[0], half[0], "ras_in", T.qas[:], T.ras[:]),
+          xfer(rl[1], half[1], "ras_in", T.qas[:], T.ras[:]))
+    n["sx"] = 2 * len(chip)
+    rid, pid = topo.addr(dm, core)
+    s = slice(128 * rank, 128 * rank + 128)
+    g.remote_dma(u8(T.la[:, s]), u8(T.qa[:]), S["a_in%d" % rank], S.sp, pid, rid, bits(far))
+    g.remote_dma(T.las[:, s], T.qas[:], S["a_in%d" % rank], S.sp, pid, rid, bits(far))
+    n["sp"] = 2 * len(far)
+
+    need(Y, "sx")
+    done(Y.dma_start(T.vt[:], T.v[:]), "ld_v", 16)
+    done(Y.dma_start(T.ut[:], T.u[:]), "ld_u", 16)
+
+    for i in (1, 2, 3):
+        q = order[i]
+        last = T.cores[q] if (q, rank) not in relay else relay[(q, rank)]
+        e = len(topo.engines(last, core))
+        n["a_in%d" % q] = 2 * e
+        n["z_in%d" % q] = 2 * e
+        n["b_in%d" % q] = e
+        n["f_in%d" % q] = e if i > 1 else len(topo.engines(last, core)[0::2])
+
+    def pen(i):
+        q = order[i]
+        if i == 0:
+            need(V, "ld_fo")
+            src = T.fbo[:]
+        else:
+            need(V, "f_in%d" % q)
+            src = T.lf[:, q:q + 1]
+        done(V.tensor_scalar(T["fn%d" % i][:], src, float(512 * rank), None, OP.subtract), "fn_ok%d" % i)
+        need(V, "fn_ok%d" % i)
+        done(V.tensor_scalar(T["pen%d" % i][:], T.num[:], T["fn%d" % i][:], LOW, OP.is_equal, OP.mult), "pen_ok%d" % i)
+
+    def score(i):
+        q = order[i]
+        if i == 0:
+            need(P, "qa_ok", "qk_ok")
+            l, ls = T.qa[:], T.qas[:]
+        else:
+            need(P, "a_in%d" % q)
+            l, ls = T.la[:, 128 * q:128 * q + 128], T.las[:, 128 * q:128 * q + 128]
+        done(P.matmul_mx(T.ps[:, 512 * i:512 * i + 512], l, ls, T.qk[:], T.qks[:], True, True), "mm_ok%d" % i)
+
+    def top(i):
+        m, r = T["ms%d" % i], T["run%d" % i]
+        need(V, "pen_ok%d" % i, "mm_ok%d" % i)
+        done(V.tensor_tensor(m[:], T.ps[:, 512 * i:512 * i + 512], T["pen%d" % i][:], OP.add), "ms_ok%d" % i)
+        need(V, "ms_ok%d" % i)
+        done(V.tensor_tensor_scan(r[:, 0:512], m[:], m[:], LOW, OP.max, OP.max), "run_ok%d" % i)
+        need(A, "run_ok%d" % i)
+        done(A.activation(T["sink%d" % i][:], r[:, 0:512], ACT.Sign, bias=r[:, 511:512], scale=-1.0,
+                          accum_out=r[:, 512:513]), "idx_ok%d" % i)
+
+    pen(0)
+    need(V, "ld_k")
+    done(V.quantize_mx(T.qk[:], T.qks[:], T.kt[:]), "qk_ok")
+    score(0)
+    top(0)
+    pen(1)
+    score(1)
+    top(1)
+    pen(2)
+    pen(3)
+    score(2)
+    score(3)
+    top(2)
+    top(3)
+
+    need(g, "idx_ok1", "idx_ok2", "idx_ok3")
+    slot = T.best[:, 4 * rank:4 * rank + 2]
+    fused("sb",
+          xfer(rl[0], bits(rest[1::2]), "rb_in", T.run2[:, 511:513], T.rbest[:]),
+          xfer(rl[1], bits(rest[0::2]), "rb_in", T.run3[:, 511:513], T.rbest[:]),
+          xfer(dm, bits(far), "b_in%d" % rank, T.run1[:, 511:513], slot))
+    n["sb"] = len(rest) + len(far)
+
+    def values(j, i0, i1):
+        x, xt, xw, o, z = T["x%d" % j], T["xt%d" % j], T["xw%d" % j], T["off%d" % j], T["z%d" % j]
+        for l, i in enumerate((i0, i1)):
+            need(V, "idx_ok%d" % i)
+            done(V.tensor_scalar(x[:, 64 * l:64 * l + 64], T.mask[:], T["run%d" % i][:, 512:513], None, OP.mult), "x_ok%d" % j)
+        need(V, "x_ok%d" % j)
+        done(V.transpose(xt[:], x[:]), "xt_ok%d" % j)
+        need(V, "xt_ok%d" % j)
+        done(V.tensor_tensor_scan(xw[:], T.keep[:], xt[:], 0.0, OP.mult, OP.add), "xw_ok%d" % j)
+        need(V, "xw_ok%d" % j)
+        for c in range(4):
+            b = 2 * (c % 2) + c // 2
+            for to in (c, c ^ 1):
+                done(V.tensor_copy(o[32 * to:32 * to + 32, b:16:4], xw[32 * c:32 * c + 32, 31:128:32]), "o1_ok%d" % j)
+        need(V, "o1_ok%d" % j)
+        done(V.tensor_copy(o[0:64, 1:16:2], o[64:128, 1:16:2]), "o2_ok%d" % j)
+        done(V.tensor_copy(o[64:128, 0:16:2], o[0:64, 0:16:2]), "o2_ok%d" % j)
+        need(V, "o2_ok%d" % j, "ld_v")
+        need(A, "o2_ok%d" % j, "ld_v")
+        for t in (0, 1):
+            done(V.tensor_copy(z[:, t:1024:4], T.vt[:, t:2048].indirect(o[:, 0:16])), "zv_ok%d" % j)
+        for t in (2, 3):
+            done(A.activation(z[:, t:1024:4], T.vt[:, t:2048].indirect(o[:, 0:16]), ACT.Copy), "zs_ok%d" % j)
+        need(V, "zv_ok%d" % j, "zs_ok%d" % j)
+        done(V.quantize_mx(T["zq%d" % j][:], T["zqs%d" % j][:], z[:]), "zq_ok%d" % j)
+
+    values(0, 2, 3)
+    need(g, "zq_ok0")
+    fused("sz",
+          xfer(rl[0], half[0], "rzc_in", u8(T.zq0[:, 0:128]), u8(T.rzc[:])),
+          xfer(rl[1], half[1], "rzc_in", u8(T.zq0[:, 128:256]), u8(T.rzc[:])))
+    fused("sz",
+          xfer(rl[0], half[0], "rzs_in", T.zqs0[:, 0:128], T.rzs[:]),
+          xfer(rl[1], half[1], "rzs_in", T.zqs0[:, 128:256], T.rzs[:]))
+    values(1, 1, 0)
+    need(g, "zq_ok1")
+    g.remote_dma(u8(T.lz[:, s]), u8(T.zq1[:, 0:128]), S["z_in%d" % rank], S.sz, pid, rid, bits(far))
+    g.remote_dma(T.lzs[:, s], T.zqs1[:, 0:128], S["z_in%d" % rank], S.sz, pid, rid, bits(far))
+    n["sz"] = 2 * len(chip) + 2 * len(far)
+
+    need(V, "ld_u")
+    done(V.quantize_mx(T.qu[:], T.qus[:], T.ut[:]), "qu_ok")
+    done(V.tensor_copy(slot, T.run0[:, 511:513]), "m1")
+    need(V, "m1", *["b_in%d" % q for q in order[1:]])
+    done(V.tensor_reduce(T.mx[:], T.best[:, 0:16:4], AxisListType.X, OP.max), "m2")
+    need(V, "m2")
+    done(V.tensor_scalar(T.t4[:], T.best[:, 0:16:4], T.mx[:], 4096.0, OP.is_lt, OP.mult), "m3")
+    need(V, "m3", "k5")
+    done(V.tensor_tensor(T.c1[:], T.t4[:], T.cq[:], OP.add), "m4")
+    done(V.tensor_tensor(T.c2[:], T.t4[:], T.nq[:], OP.add), "m4")
+    need(V, "m4")
+    done(V.tensor_reduce(T.pick[:], T.c1[:], AxisListType.X, OP.min), "pick_ok")
+    done(V.tensor_tensor(T.c3[:], T.c2[:], T.best[:, 1:16:4], OP.add), "m5")
+    need(V, "pick_ok", "m5")
+    done(V.tensor_scalar(T.xf[:], T.mask[:], T.pick[:], 0.25, OP.mult, OP.mult), "xf_ok")
+    done(V.tensor_reduce(T.won[:], T.c3[:], AxisListType.X, OP.min), "won_ok")
+    need(Y, "won_ok")
+    done(Y.dma_start(T.win[:], T.won[:]), "st", 16)
+    need(V, "xf_ok")
+    done(V.transpose(T.yf[:], T.xf[:]), "yf_ok")
+    need(V, "yf_ok")
+    done(V.tensor_tensor_scan(T.wf[:], T.keep[:, 0:64], T.yf[:], 0.0, OP.mult, OP.add), "wf_ok")
+    need(V, "wf_ok")
+    for c in range(4):
+        for to in (c, c ^ 1):
+            done(V.tensor_copy(T.of[32 * to:32 * to + 32, 2 * c:2 * c + 2], T.wf[32 * c:32 * c + 32, 31:64:32]), "of1_ok")
+    need(V, "of1_ok")
+    done(V.tensor_copy(T.of[0:64, 4:8], T.of[64:128, 4:8]), "of2_ok")
+    done(V.tensor_copy(T.of[64:128, 0:4], T.of[0:64, 0:4]), "of2_ok")
+
+    for i in range(4):
+        q = order[i]
+        if i == 0:
+            need(P, "qu_ok", "zq_ok1")
+            r, rs = T.zq1[:, 128:256], T.zqs1[:, 128:256]
+        else:
+            need(P, "z_in%d" % q)
+            r, rs = T.lz[:, 128 * q:128 * q + 128], T.lzs[:, 128 * q:128 * q + 128]
+        done(P.matmul_mx(T.pu[:, 512 * i:512 * i + 128], T.qu[:], T.qus[:], r, rs, True, True), "pu_ok%d" % i)
+        to, frm = T.prod[:, 128 * q:128 * q + 128], T.pu[:, 512 * i:512 * i + 128]
+        if i in (0, 2):
+            need(V, "pu_ok%d" % i)
+            done(V.tensor_copy(to, frm), "uv")
+        else:
+            need(A, "pu_ok%d" % i)
+            done(A.activation(to, frm, ACT.Copy), "us")
+    need(V, "of2_ok", "uv", "us")
+    done(V.tensor_copy(T.ysb[:], T.prod[:].indirect(T.of[:, 0:8])), "y_ok")
+    need(Y, "y_ok")
+    done(Y.dma_start(T.y[:], T.ysb[:]), "st", 16)
+    need(Y, "st")
+    need(g, "sf", "sp", "sb", "sz")
+
+
+def relay_program(g, core, T, topo, r, d):
+    S = T.sem
+    dst = T.cores[d]
+    rid, pid = topo.addr(dst, core)
+    m = topo.mask(core, dst)
+    e = len(topo.engines(core, dst))
+    src = T.cores[r]
+    chip = topo.engines(src, core)
+    rest = [x for x in chip if x not in topo.engines(src, [c for i, c in enumerate(T.cores) if i != r and topo.may_write(src, c)][0])]
+    s = slice(128 * r, 128 * r + 128)
+    hops = [
+        ("rf_in", 2, T.lf[:, r:r + 1], T.rfb[:], "f_in"),
+        ("rac_in", len(chip) // 2, u8(T.la[:, s]), u8(T.rac[:]), "a_in"),
+        ("ras_in", len(chip) // 2, T.las[:, s], T.ras[:], "a_in"),
+        ("rb_in", len(rest) // 2, T.best[:, 4 * r:4 * r + 2], T.rbest[:], "b_in"),
+        ("rzc_in", len(chip) // 2, u8(T.lz[:, s]), u8(T.rzc[:]), "z_in"),
+        ("rzs_in", len(chip) // 2, T.lzs[:, s], T.rzs[:], "z_in"),
+    ]
+    for sem, k, to, frm, there in hops:
+        g.wait_ge(S[sem], k)
+        g.remote_dma(to, frm, S["%s%d" % (there, r)], S.rsent, pid, rid, m)
+    g.wait_ge(S.rsent, len(hops) * e)

@@ -4,7 +4,7 @@ from concourse.mybir import dt, AluOpType, AxisListType, ActivationFunctionType
 OP = AluOpType
 ACT = ActivationFunctionType
 C8 = "float8_e4m3fn_x4"
-LOW = -1.0e29
+FAR = 1.0e29
 
 SCRATCH = {
     "at": ("sbuf", [128, 512], "bfloat16"),
@@ -20,6 +20,7 @@ SCRATCH = {
     "lf": ("sbuf", [128, 4], "int32"),
     "best": ("sbuf", [128, 16], "float32"),
     "lz": ("sbuf", [128, 512], C8), "lzs": ("sbuf", [128, 512], "uint8"),
+    "lc": ("sbuf", [128, 4], "float32"), "ln": ("sbuf", [128, 4], "float32"),
     "rfb": ("dram", [128, 1], "int32"),
     "rac": ("sbuf", [128, 128], C8), "ras": ("sbuf", [128, 128], "uint8"),
     "rbest": ("sbuf", [128, 2], "float32"),
@@ -51,6 +52,7 @@ for _i in range(4):
     SCRATCH["run%d" % _i] = ("sbuf", [128, 520], "float32")
     SCRATCH["sink%d" % _i] = ("sbuf", [128, 512], "bfloat16")
 for _j in range(2):
+    SCRATCH["ab%d" % (_j + 2)] = ("sbuf", [128, 512], "bfloat16")
     SCRATCH["x%d" % _j] = ("sbuf", [128, 128], "float32")
     SCRATCH["xt%d" % _j] = ("sbuf", [128, 128], "float32")
     SCRATCH["xw%d" % _j] = ("sbuf", [128, 128], "float32")
@@ -62,9 +64,9 @@ for _j in range(2):
 SEMAPHORES = (
     ["ld_a", "ld_k", "ld_v", "ld_u", "ld_fd", "ld_fo", "st"]
     + ["sf", "sx", "sp", "sb", "sz"]
-    + ["rf_in", "rac_in", "ras_in", "rb_in", "rzc_in", "rzs_in", "rsent"]
+    + ["rf_in", "rac_in", "ras_in", "rb_in", "rzc_in", "rzs_in", "rsent", "lc_in", "ln_in"]
     + ["%s%d" % (n, i) for n in ("a_in", "f_in", "b_in", "z_in") for i in range(4)]
-    + ["io", "k1", "k2", "k3", "k4", "k5", "qa_ok", "qk_ok", "qu_ok"]
+    + ["k0", "k1", "k2", "k3", "k4", "k5", "qa_ok", "qk_ok", "qu_ok", "ab_ok2", "ab_ok3", "half2"]
     + ["%s%d" % (n, i) for n in ("fn_ok", "pen_ok", "mm_ok", "ms_ok", "run_ok", "idx_ok", "pu_ok") for i in range(4)]
     + ["%s%d" % (n, j) for n in ("x_ok", "xt_ok", "xw_ok", "o1_ok", "o2_ok", "zv_ok", "zs_ok", "zq_ok") for j in range(2)]
     + ["m1", "m2", "m3", "m4", "m5", "pick_ok", "won_ok", "xf_ok", "yf_ok", "wf_ok", "of1_ok", "of2_ok", "uv", "us", "y_ok"]
@@ -100,7 +102,7 @@ def rank_program(g, core, T, topo):
     if rank is None:
         for (r, d), c in relay.items():
             if c == core:
-                relay_program(g, core, T, topo, r, d)
+                relay_program(g, core, T, topo, r, d, min(q for q, b in relay if b == d) == r)
         return
     S = T.sem
     V, P, A, Y = g.vector, g.tensor, g.scalar, g.sync
@@ -124,29 +126,18 @@ def rank_program(g, core, T, topo):
     done(A.dma_start(T.fbo[:], T.fb[:]), "ld_fo", 16)
     done(Y.dma_start(T.kt[:], T.k[:]), "ld_k", 16)
 
-    done(g.iota(T.im[:], [[-16, 2], [0, 2], [-1, 16]], 64, 1), "io")
-    done(g.iota(T.ip[:], [[0, 4]], 0, 1), "io")
-    done(g.iota(T.cp[:], [[128, 4]], 0, 1, allow_small_or_imprecise_dtypes=True), "io")
-    done(g.iota(T.nq[:], [[512, 4]], 0, 0, allow_small_or_imprecise_dtypes=True), "io")
+    done(g.iota(T.im[:], [[-16, 2], [0, 2], [-1, 16]], 64, 1), "k0")
     done(V.memset(T.ones[:], 1.0), "k1")
     done(V.memset(T.keep[:], 1.0), "k1")
     need(V, "k1")
     done(V.tensor_tensor_scan(T.num[:], T.ones[:], T.ones[:], -1.0, OP.add, OP.mult), "k2")
     done(V.memset(T.keep[:, 0:128:32], 0.0), "k2")
-    need(V, "io")
-    done(V.tensor_scalar(T.am[:], T.im[:], 31, None, OP.bitwise_and), "k3")
-    done(V.tensor_scalar(T.i1[:], T.ip[:], 4, 1, OP.arith_shift_right, OP.bitwise_and), "k3")
-    done(V.tensor_scalar(T.i2[:], T.ip[:], 6, None, OP.arith_shift_right), "k3")
-    need(V, "k2", "k3")
-    done(V.tensor_scalar(T.mask[:], T.am[:], 0.0, 4.0, OP.is_equal, OP.mult), "k4")
-    done(V.tensor_tensor(T.i3[:], T.i1[:], T.i2[:], OP.subtract), "k4")
-    need(V, "k4")
-    done(V.tensor_scalar(T.cd[:], T.i3[:], 48.0, None, OP.mult), "k5")
-    need(V, "k5")
-    done(V.tensor_tensor(T.cq[:], T.cp[:], T.cd[:], OP.add), "k5")
-
     need(V, "ld_a")
     done(V.quantize_mx(T.qa[:], T.qas[:], T.at[:]), "qa_ok")
+    need(V, "k0")
+    done(V.tensor_scalar(T.am[:], T.im[:], 31, None, OP.bitwise_and), "k3")
+    need(V, "k3")
+    done(V.tensor_scalar(T.mask[:], T.am[:], 0.0, 4.0, OP.is_equal, OP.mult), "k4")
 
     far = topo.engines(core, T.cores[mate])
     chip = topo.engines(core, relay[(rank, cross[0])])
@@ -194,8 +185,10 @@ def rank_program(g, core, T, topo):
         n["z_in%d" % q] = 2 * e
         n["b_in%d" % q] = e
         n["f_in%d" % q] = e if i > 1 else len(topo.engines(last, core)[0::2])
+        if i > 1:
+            n["lc_in"] = n["ln_in"] = e
 
-    def pen(i):
+    def forbidden(i):
         q = order[i]
         if i == 0:
             need(V, "ld_fo")
@@ -204,40 +197,64 @@ def rank_program(g, core, T, topo):
             need(V, "f_in%d" % q)
             src = T.lf[:, q:q + 1]
         done(V.tensor_scalar(T["fn%d" % i][:], src, float(512 * rank), None, OP.subtract), "fn_ok%d" % i)
-        need(V, "fn_ok%d" % i)
-        done(V.tensor_scalar(T["pen%d" % i][:], T.num[:], T["fn%d" % i][:], LOW, OP.is_equal, OP.mult), "pen_ok%d" % i)
 
-    def score(i):
+    def pen_v(i):
+        need(V, "fn_ok%d" % i, "k2")
+        done(V.tensor_scalar(T["pen%d" % i][:], T.num[:], T["fn%d" % i][:], FAR, OP.is_equal, OP.mult), "pen_ok%d" % i)
+
+    def pen_a(i):
+        need(A, "fn_ok%d" % i, "k2")
+        done(A.activation(T["ab%d" % i][:], T.num[:], ACT.Abs, bias=T["fn%d" % i][:], scale=-1.0), "ab_ok%d" % i)
+        need(A, "ab_ok%d" % i)
+        done(A.activation(T["pen%d" % i][:], T["ab%d" % i][:], ACT.Relu, bias=FAR, scale=-FAR), "pen_ok%d" % i)
+
+    def anchors(i):
         q = order[i]
         if i == 0:
             need(P, "qa_ok", "qk_ok")
-            l, ls = T.qa[:], T.qas[:]
-        else:
-            need(P, "a_in%d" % q)
-            l, ls = T.la[:, 128 * q:128 * q + 128], T.las[:, 128 * q:128 * q + 128]
+            return T.qa[:], T.qas[:]
+        need(P, "a_in%d" % q)
+        return T.la[:, 128 * q:128 * q + 128], T.las[:, 128 * q:128 * q + 128]
+
+    def score(i):
+        l, ls = anchors(i)
         done(P.matmul_mx(T.ps[:, 512 * i:512 * i + 512], l, ls, T.qk[:], T.qks[:], True, True), "mm_ok%d" % i)
 
+    def halves(i):
+        l, ls = anchors(i)
+        done(P.matmul_mx(T.ps[:, 512 * i:512 * i + 256], l, ls, T.qk[:, 0:256], T.qks[:, 0:256], True, True), "mm_ok%d" % i)
+        done(P.matmul_mx(T.pu[:, 512 * i:512 * i + 256], l, ls, T.qk[:, 256:512], T.qks[:, 256:512], True, True), "half%d" % i)
+
     def top(i):
-        m, r = T["ms%d" % i], T["run%d" % i]
+        m, r, p = T["ms%d" % i], T["run%d" % i], T["pen%d" % i]
         need(V, "pen_ok%d" % i, "mm_ok%d" % i)
-        done(V.tensor_tensor(m[:], T.ps[:, 512 * i:512 * i + 512], T["pen%d" % i][:], OP.add), "ms_ok%d" % i)
+        if i == 2:
+            done(V.tensor_tensor(m[:, 0:256], T.ps[:, 512 * i:512 * i + 256], p[:, 0:256], OP.subtract), "ms_ok%d" % i)
+            need(V, "half%d" % i)
+            done(V.tensor_tensor(m[:, 256:512], T.pu[:, 512 * i:512 * i + 256], p[:, 256:512], OP.subtract), "ms_ok%d" % i)
+        else:
+            done(V.tensor_tensor(m[:], T.ps[:, 512 * i:512 * i + 512], p[:], OP.subtract), "ms_ok%d" % i)
         need(V, "ms_ok%d" % i)
-        done(V.tensor_tensor_scan(r[:, 0:512], m[:], m[:], LOW, OP.max, OP.max), "run_ok%d" % i)
+        done(V.tensor_tensor_scan(r[:, 0:512], m[:], m[:], -FAR, OP.max, OP.max), "run_ok%d" % i)
         need(A, "run_ok%d" % i)
         done(A.activation(T["sink%d" % i][:], r[:, 0:512], ACT.Sign, bias=r[:, 511:512], scale=-1.0,
                           accum_out=r[:, 512:513]), "idx_ok%d" % i)
 
-    pen(0)
+    forbidden(0)
+    pen_v(0)
     need(V, "ld_k")
     done(V.quantize_mx(T.qk[:], T.qks[:], T.kt[:]), "qk_ok")
     score(0)
     top(0)
-    pen(1)
+    forbidden(1)
+    pen_v(1)
+    forbidden(2)
+    forbidden(3)
+    pen_a(2)
+    pen_a(3)
     score(1)
     top(1)
-    pen(2)
-    pen(3)
-    score(2)
+    halves(2)
     score(3)
     top(2)
     top(3)
@@ -253,7 +270,7 @@ def rank_program(g, core, T, topo):
     def values(j, i0, i1):
         x, xt, xw, o, z = T["x%d" % j], T["xt%d" % j], T["xw%d" % j], T["off%d" % j], T["z%d" % j]
         for l, i in enumerate((i0, i1)):
-            need(V, "idx_ok%d" % i)
+            need(V, "idx_ok%d" % i, "k4")
             done(V.tensor_scalar(x[:, 64 * l:64 * l + 64], T.mask[:], T["run%d" % i][:, 512:513], None, OP.mult), "x_ok%d" % j)
         need(V, "x_ok%d" % j)
         done(V.transpose(xt[:], x[:]), "xt_ok%d" % j)
@@ -297,9 +314,9 @@ def rank_program(g, core, T, topo):
     done(V.tensor_reduce(T.mx[:], T.best[:, 0:16:4], AxisListType.X, OP.max), "m2")
     need(V, "m2")
     done(V.tensor_scalar(T.t4[:], T.best[:, 0:16:4], T.mx[:], 4096.0, OP.is_lt, OP.mult), "m3")
-    need(V, "m3", "k5")
-    done(V.tensor_tensor(T.c1[:], T.t4[:], T.cq[:], OP.add), "m4")
-    done(V.tensor_tensor(T.c2[:], T.t4[:], T.nq[:], OP.add), "m4")
+    need(V, "m3", "lc_in", "ln_in")
+    done(V.tensor_tensor(T.c1[:], T.t4[:], T.lc[:], OP.add), "m4")
+    done(V.tensor_tensor(T.c2[:], T.t4[:], T.ln[:], OP.add), "m4")
     need(V, "m4")
     done(V.tensor_reduce(T.pick[:], T.c1[:], AxisListType.X, OP.min), "pick_ok")
     done(V.tensor_tensor(T.c3[:], T.c2[:], T.best[:, 1:16:4], OP.add), "m5")
@@ -328,6 +345,8 @@ def rank_program(g, core, T, topo):
         else:
             need(P, "z_in%d" % q)
             r, rs = T.lz[:, 128 * q:128 * q + 128], T.lzs[:, 128 * q:128 * q + 128]
+        if i == 2:
+            need(P, "ms_ok2")
         done(P.matmul_mx(T.pu[:, 512 * i:512 * i + 128], T.qu[:], T.qus[:], r, rs, True, True), "pu_ok%d" % i)
         to, frm = T.prod[:, 128 * q:128 * q + 128], T.pu[:, 512 * i:512 * i + 128]
         if i in (0, 2):
@@ -344,12 +363,31 @@ def rank_program(g, core, T, topo):
     need(g, "sf", "sp", "sb", "sz")
 
 
-def relay_program(g, core, T, topo, r, d):
+def relay_program(g, core, T, topo, r, d, place):
     S = T.sem
+    V = g.vector
     dst = T.cores[d]
     rid, pid = topo.addr(dst, core)
     m = topo.mask(core, dst)
     e = len(topo.engines(core, dst))
+    if place:
+        g.iota(T.ip[:], [[0, 4]], 0, 1).then_inc(S.k0, 1)
+        g.iota(T.cp[:], [[128, 4]], 0, 1, allow_small_or_imprecise_dtypes=True).then_inc(S.k0, 1)
+        V.wait_ge(S.k0, 2)
+        V.tensor_scalar(T.i1[:], T.ip[:], 4, 1, OP.arith_shift_right, OP.bitwise_and).then_inc(S.k3, 1)
+        V.tensor_scalar(T.i2[:], T.ip[:], 6, None, OP.arith_shift_right).then_inc(S.k3, 1)
+        V.wait_ge(S.k3, 2)
+        V.tensor_tensor(T.i3[:], T.i1[:], T.i2[:], OP.subtract).then_inc(S.k4, 1)
+        V.wait_ge(S.k4, 1)
+        V.tensor_scalar(T.cd[:], T.i3[:], 48.0, None, OP.mult).then_inc(S.k5, 1)
+        V.wait_ge(S.k5, 1)
+        V.tensor_tensor(T.cq[:], T.cp[:], T.cd[:], OP.add).then_inc(S.k1, 1)
+        g.wait_ge(S.k1, 1)
+        g.remote_dma(T.lc[:], T.cq[:], S.lc_in, S.rsent, pid, rid, m)
+    else:
+        g.iota(T.nq[:], [[512, 4]], 0, 0, allow_small_or_imprecise_dtypes=True).then_inc(S.k0, 1)
+        g.wait_ge(S.k0, 1)
+        g.remote_dma(T.ln[:], T.nq[:], S.ln_in, S.rsent, pid, rid, m)
     src = T.cores[r]
     chip = topo.engines(src, core)
     rest = [x for x in chip if x not in topo.engines(src, [c for i, c in enumerate(T.cores) if i != r and topo.may_write(src, c)][0])]
@@ -365,4 +403,4 @@ def relay_program(g, core, T, topo, r, d):
     for sem, k, to, frm, there in hops:
         g.wait_ge(S[sem], k)
         g.remote_dma(to, frm, S["%s%d" % (there, r)], S.rsent, pid, rid, m)
-    g.wait_ge(S.rsent, len(hops) * e)
+    g.wait_ge(S.rsent, (1 + len(hops)) * e)

from concourse.bass import DstId, RemoteDMATransfer
from concourse.mybir import dt, AluOpType, AxisListType, ActivationFunctionType

OP = AluOpType
ACT = ActivationFunctionType
C8 = "float8_e4m3fn_x4"
FAR = 1.0e29

SCRATCH = {
    "at": ("sbuf", [128, 512], "bfloat16"),
    "kt": ("sbuf", [128, 2048], "bfloat16"),
    "vt": ("sbuf", [128, 2048], "bfloat16"),
    "ut": ("sbuf", [128, 512], "bfloat16"),
    "fbd": ("dram", [128, 1], "int32"),
    "fbo": ("sbuf", [128, 1], "int32"),
    "qa": ("sbuf", [128, 128], C8), "qas": ("sbuf", [128, 128], "uint8"),
    "qk": ("sbuf", [128, 512], C8), "qks": ("sbuf", [128, 512], "uint8"),
    "qu": ("sbuf", [128, 128], C8), "qus": ("sbuf", [128, 128], "uint8"),
    "la": ("sbuf", [128, 512], C8), "las": ("sbuf", [128, 512], "uint8"),
    "lf": ("sbuf", [128, 4], "int32"),
    "best": ("sbuf", [128, 16], "float32"),
    "lz": ("sbuf", [128, 512], C8), "lzs": ("sbuf", [128, 512], "uint8"),
    "lc": ("sbuf", [128, 4], "float32"), "ln": ("sbuf", [128, 4], "float32"),
    "rfb": ("dram", [128, 1], "int32"),
    "rac": ("sbuf", [128, 128], C8), "ras": ("sbuf", [128, 128], "uint8"),
    "rbest": ("sbuf", [128, 2], "float32"),
    "rzc": ("sbuf", [128, 128], C8), "rzs": ("sbuf", [128, 128], "uint8"),
    "ones": ("sbuf", [128, 512], "float32"),
    "num": ("sbuf", [128, 512], "float32"),
    "im": ("sbuf", [128, 64], "int32"), "am": ("sbuf", [128, 64], "int32"),
    "mask": ("sbuf", [128, 64], "float32"),
    "keep": ("sbuf", [128, 128], "float32"),
    "ip": ("sbuf", [128, 4], "int32"), "i1": ("sbuf", [128, 4], "int32"),
    "i2": ("sbuf", [128, 4], "int32"), "i3": ("sbuf", [128, 4], "int32"),
    "cp": ("sbuf", [128, 4], "float32"), "cd": ("sbuf", [128, 4], "float32"),
    "cq": ("sbuf", [128, 4], "float32"), "nq": ("sbuf", [128, 4], "float32"),
    "mx": ("sbuf", [128, 1], "float32"), "t4": ("sbuf", [128, 4], "float32"),
    "c1": ("sbuf", [128, 4], "float32"), "c2": ("sbuf", [128, 4], "float32"),
    "c3": ("sbuf", [128, 4], "float32"),
    "pick": ("sbuf", [128, 1], "float32"), "won": ("sbuf", [128, 1], "float32"),
    "xf": ("sbuf", [128, 64], "float32"), "yf": ("sbuf", [128, 64], "float32"),
    "wf": ("sbuf", [128, 64], "float32"), "of": ("sbuf", [128, 8], "uint16"),
    "prod": ("sbuf", [128, 512], "float32"),
    "ysb": ("sbuf", [128, 128], "float32"),
    "ps": ("psum", [128, 2048], "float32"),
    "pu": ("psum", [128, 2048], "float32"),
}
for _i in range(4):
    SCRATCH["fn%d" % _i] = ("sbuf", [128, 1], "float32")
    SCRATCH["pen%d" % _i] = ("sbuf", [128, 512], "float32")
    SCRATCH["ms%d" % _i] = ("sbuf", [128, 512], "float32")
    SCRATCH["run%d" % _i] = ("sbuf", [128, 520], "float32")
    SCRATCH["sink%d" % _i] = ("sbuf", [128, 512], "bfloat16")
for _j in range(2):
    SCRATCH["ab%d" % (_j + 2)] = ("sbuf", [128, 512], "bfloat16")
    SCRATCH["x%d" % _j] = ("sbuf", [128, 128], "float32")
    SCRATCH["xt%d" % _j] = ("sbuf", [128, 128], "float32")
    SCRATCH["xw%d" % _j] = ("sbuf", [128, 128], "float32")
    SCRATCH["off%d" % _j] = ("sbuf", [128, 16], "uint16")
    SCRATCH["z%d" % _j] = ("sbuf", [128, 1024], "bfloat16")
    SCRATCH["zq%d" % _j] = ("sbuf", [128, 256], C8)
    SCRATCH["zqs%d" % _j] = ("sbuf", [128, 256], "uint8")

SEMAPHORES = (
    ["ld_a", "ld_k", "ld_v", "ld_u", "ld_fd", "ld_fo", "st"]
    + ["sf", "sx", "sp", "sb", "sz"]
    + ["rf_in", "rac_in", "ras_in", "rb_in", "rzc_in", "rzs_in", "rsent", "lc_in", "ln_in"]
    + ["%s%d" % (n, i) for n in ("a_in", "f_in", "b_in", "z_in") for i in range(4)]
    + ["k0", "k1", "k2", "k3", "k4", "k5", "qa_ok", "qk_ok", "qu_ok", "ab_ok2", "ab_ok3", "half2"]
    + ["%s%d" % (n, i) for n in ("fn_ok", "pen_ok", "mm_ok", "ms_ok", "run_ok", "idx_ok", "pu_ok") for i in range(4)]
    + ["%s%d" % (n, j) for n in ("x_ok", "xt_ok", "xw_ok", "o1_ok", "o2_ok", "zv_ok", "zs_ok", "zq_ok") for j in range(2)]
    + ["m1", "m2", "m3", "m4", "m5", "pick_ok", "won_ok", "xf_ok", "yf_ok", "wf_ok", "of1_ok", "of2_ok", "uv", "us", "y_ok"]
)


def bits(engines):
    m = 0
    for e in engines:
        m |= 1 << e
    return m


def roads(T, topo):
    relay = {}
    for r, a in enumerate(T.cores):
        for d, b in enumerate(T.cores):
            if d == r or topo.may_write(a, b):
                continue
            near = topo.host(a) == topo.host(b)
            c = [x for x in topo.cores_of(a) if x != a and topo.may_write(x, b) and (topo.die(x) == topo.die(a)) == near]
            relay[(r, d)] = c[0]
    return relay


def u8(view):
    return view.bitcast(dt.uint8)


def rank_program(g, core, T, topo):
    relay = roads(T, topo)
    rank = T.rank_of(core)
    if rank is None:
        for (r, d), c in relay.items():
            if c == core:
                relay_program(g, core, T, topo, r, d, min(q for q, b in relay if b == d) == r)
        return
    S = T.sem
    V, P, A, Y = g.vector, g.tensor, g.scalar, g.sync
    direct = [d for d in range(len(T.cores)) if d != rank and (rank, d) not in relay]
    cross = [d for d in range(len(T.cores)) if (rank, d) in relay]
    cross.sort(key=lambda d: topo.die(relay[(rank, d)]) != topo.die(core))
    mate = direct[0]
    order = [rank, mate] + cross
    n = {}

    def done(q, name, k=1):
        q.then_inc(S[name], k)
        n[name] = n.get(name, 0) + k

    def need(queue, *names):
        for x in names:
            queue.wait_ge(S[x], n[x])

    done(Y.dma_start(T.at[:], T.an[:]), "ld_a", 16)
    done(A.dma_start(T.fbd[:], T.fb[:]), "ld_fd", 16)
    done(A.dma_start(T.fbo[:], T.fb[:]), "ld_fo", 16)
    done(Y.dma_start(T.kt[:], T.k[:]), "ld_k", 16)

    done(g.iota(T.im[:], [[-16, 2], [0, 2], [-1, 16]], 64, 1), "k0")
    done(V.memset(T.ones[:], 1.0), "k1")
    done(V.memset(T.keep[:], 1.0), "k1")
    need(V, "k1")
    done(V.tensor_tensor_scan(T.num[:], T.ones[:], T.ones[:], -1.0, OP.add, OP.mult), "k2")
    done(V.memset(T.keep[:, 0:128:32], 0.0), "k2")
    need(V, "ld_a")
    done(V.quantize_mx(T.qa[:], T.qas[:], T.at[:]), "qa_ok")
    need(V, "k0")
    done(V.tensor_scalar(T.am[:], T.im[:], 31, None, OP.bitwise_and), "k3")
    need(V, "k3")
    done(V.tensor_scalar(T.mask[:], T.am[:], 0.0, 4.0, OP.is_equal, OP.mult), "k4")

    far = topo.engines(core, T.cores[mate])
    chip = topo.engines(core, relay[(rank, cross[0])])
    rest = [e for e in chip if e not in far]

    def xfer(dst, mask, sem, src, to):
        rid, pid = topo.addr(dst, core)
        return RemoteDMATransfer(dst_ids=[DstId(rid=rid, pnc=pid)], dma_engine_mask=mask, remote_sem=S[sem], src=src, dst=to)

    def fused(sem, *ts):
        g.remote_dma_fused(list(ts), local_sem=S[sem])

    rl = [relay[(rank, d)] for d in cross]
    dm = T.cores[mate]
    half = [bits(chip[1::2]), bits(chip[0::2])]
    need(g, "ld_fd")
    fused("sf",
          xfer(rl[0], bits(rest[0:2]), "rf_in", T.fbd[:], T.rfb[:]),
          xfer(rl[1], bits(rest[2:4]), "rf_in", T.fbd[:], T.rfb[:]),
          xfer(dm, bits(far[0::2]), "f_in%d" % rank, T.fbd[:], T.lf[:, rank:rank + 1]))
    n["sf"] = 2 + 2 + len(far[0::2])
    need(g, "qa_ok")
    fused("sx",
          xfer(rl[0], half[0], "rac_in", u8(T.qa[:]), u8(T.rac[:])),
          xfer(rl[1], half[1], "rac_in", u8(T.qa[:]), u8(T.rac[:])))
    fused("sx",
          xfer(rl[0], half[0], "ras_in", T.qas[:], T.ras[:]),
          xfer(rl[1], half[1], "ras_in", T.qas[:], T.ras[:]))
    n["sx"] = 2 * len(chip)
    rid, pid = topo.addr(dm, core)
    s = slice(128 * rank, 128 * rank + 128)
    g.remote_dma(u8(T.la[:, s]), u8(T.qa[:]), S["a_in%d" % rank], S.sp, pid, rid, bits(far))
    g.remote_dma(T.las[:, s], T.qas[:], S["a_in%d" % rank], S.sp, pid, rid, bits(far))
    n["sp"] = 2 * len(far)

    need(Y, "sx")
    done(Y.dma_start(T.vt[:], T.v[:]), "ld_v", 16)
    done(Y.dma_start(T.ut[:], T.u[:]), "ld_u", 16)

    for i in (1, 2, 3):
        q = order[i]
        last = T.cores[q] if (q, rank) not in relay else relay[(q, rank)]
        e = len(topo.engines(last, core))
        n["a_in%d" % q] = 2 * e
        n["z_in%d" % q] = 2 * e
        n["b_in%d" % q] = e
        n["f_in%d" % q] = e if i > 1 else len(topo.engines(last, core)[0::2])
        if i > 1:
            n["lc_in"] = n["ln_in"] = e

    def forbidden(i):
        q = order[i]
        if i == 0:
            need(V, "ld_fo")
            src = T.fbo[:]
        else:
            need(V, "f_in%d" % q)
            src = T.lf[:, q:q + 1]
        done(V.tensor_scalar(T["fn%d" % i][:], src, float(512 * rank), None, OP.subtract), "fn_ok%d" % i)

    def pen_v(i):
        need(V, "fn_ok%d" % i, "k2")
        done(V.tensor_scalar(T["pen%d" % i][:], T.num[:], T["fn%d" % i][:], FAR, OP.is_equal, OP.mult), "pen_ok%d" % i)

    def pen_a(i):
        need(A, "fn_ok%d" % i, "k2")
        done(A.activation(T["ab%d" % i][:], T.num[:], ACT.Abs, bias=T["fn%d" % i][:], scale=-1.0), "ab_ok%d" % i)
        need(A, "ab_ok%d" % i)
        done(A.activation(T["pen%d" % i][:], T["ab%d" % i][:], ACT.Relu, bias=FAR, scale=-FAR), "pen_ok%d" % i)

    def anchors(i):
        q = order[i]
        if i == 0:
            need(P, "qa_ok", "qk_ok")
            return T.qa[:], T.qas[:]
        need(P, "a_in%d" % q)
        return T.la[:, 128 * q:128 * q + 128], T.las[:, 128 * q:128 * q + 128]

    def score(i):
        l, ls = anchors(i)
        done(P.matmul_mx(T.ps[:, 512 * i:512 * i + 512], l, ls, T.qk[:], T.qks[:], True, True), "mm_ok%d" % i)

    def halves(i):
        l, ls = anchors(i)
        done(P.matmul_mx(T.ps[:, 512 * i:512 * i + 256], l, ls, T.qk[:, 0:256], T.qks[:, 0:256], True, True), "mm_ok%d" % i)
        done(P.matmul_mx(T.pu[:, 512 * i:512 * i + 256], l, ls, T.qk[:, 256:512], T.qks[:, 256:512], True, True), "half%d" % i)

    def top(i):
        m, r, p = T["ms%d" % i], T["run%d" % i], T["pen%d" % i]
        need(V, "pen_ok%d" % i, "mm_ok%d" % i)
        if i == 2:
            done(V.tensor_tensor(m[:, 0:256], T.ps[:, 512 * i:512 * i + 256], p[:, 0:256], OP.subtract), "ms_ok%d" % i)
            need(V, "half%d" % i)
            done(V.tensor_tensor(m[:, 256:512], T.pu[:, 512 * i:512 * i + 256], p[:, 256:512], OP.subtract), "ms_ok%d" % i)
        else:
            done(V.tensor_tensor(m[:], T.ps[:, 512 * i:512 * i + 512], p[:], OP.subtract), "ms_ok%d" % i)
        need(V, "ms_ok%d" % i)
        done(V.tensor_tensor_scan(r[:, 0:512], m[:], m[:], -FAR, OP.max, OP.max), "run_ok%d" % i)
        need(A, "run_ok%d" % i)
        done(A.activation(T["sink%d" % i][:], r[:, 0:512], ACT.Sign, bias=r[:, 511:512], scale=-1.0,
                          accum_out=r[:, 512:513]), "idx_ok%d" % i)

    forbidden(0)
    pen_v(0)
    need(V, "ld_k")
    done(V.quantize_mx(T.qk[:], T.qks[:], T.kt[:]), "qk_ok")
    score(0)
    top(0)
    forbidden(1)
    pen_v(1)
    forbidden(2)
    forbidden(3)
    pen_a(2)
    pen_a(3)
    score(1)
    top(1)
    halves(2)
    score(3)
    top(2)
    top(3)

    need(g, "idx_ok1", "idx_ok2", "idx_ok3")
    slot = T.best[:, 4 * rank:4 * rank + 2]
    fused("sb",
          xfer(rl[0], bits(rest[1::2]), "rb_in", T.run2[:, 511:513], T.rbest[:]),
          xfer(rl[1], bits(rest[0::2]), "rb_in", T.run3[:, 511:513], T.rbest[:]),
          xfer(dm, bits(far), "b_in%d" % rank, T.run1[:, 511:513], slot))
    n["sb"] = len(rest) + len(far)

    def values(j, i0, i1):
        x, xt, xw, o, z = T["x%d" % j], T["xt%d" % j], T["xw%d" % j], T["off%d" % j], T["z%d" % j]
        for l, i in enumerate((i0, i1)):
            need(V, "idx_ok%d" % i, "k4")
            done(V.tensor_scalar(x[:, 64 * l:64 * l + 64], T.mask[:], T["run%d" % i][:, 512:513], None, OP.mult), "x_ok%d" % j)
        need(V, "x_ok%d" % j)
        done(V.transpose(xt[:], x[:]), "xt_ok%d" % j)
        need(V, "xt_ok%d" % j)
        done(V.tensor_tensor_scan(xw[:], T.keep[:], xt[:], 0.0, OP.mult, OP.add), "xw_ok%d" % j)
        need(V, "xw_ok%d" % j)
        for c in range(4):
            b = 2 * (c % 2) + c // 2
            for to in (c, c ^ 1):
                done(V.tensor_copy(o[32 * to:32 * to + 32, b:16:4], xw[32 * c:32 * c + 32, 31:128:32]), "o1_ok%d" % j)
        need(V, "o1_ok%d" % j)
        done(V.tensor_copy(o[0:64, 1:16:2], o[64:128, 1:16:2]), "o2_ok%d" % j)
        done(V.tensor_copy(o[64:128, 0:16:2], o[0:64, 0:16:2]), "o2_ok%d" % j)
        need(V, "o2_ok%d" % j, "ld_v")
        need(A, "o2_ok%d" % j, "ld_v")
        for t in (0, 1):
            done(V.tensor_copy(z[:, t:1024:4], T.vt[:, t:2048].indirect(o[:, 0:16])), "zv_ok%d" % j)
        for t in (2, 3):
            done(A.activation(z[:, t:1024:4], T.vt[:, t:2048].indirect(o[:, 0:16]), ACT.Copy), "zs_ok%d" % j)
        need(V, "zv_ok%d" % j, "zs_ok%d" % j)
        done(V.quantize_mx(T["zq%d" % j][:], T["zqs%d" % j][:], z[:]), "zq_ok%d" % j)

    values(0, 2, 3)
    need(g, "zq_ok0")
    fused("sz",
          xfer(rl[0], half[0], "rzc_in", u8(T.zq0[:, 0:128]), u8(T.rzc[:])),
          xfer(rl[1], half[1], "rzc_in", u8(T.zq0[:, 128:256]), u8(T.rzc[:])))
    fused("sz",
          xfer(rl[0], half[0], "rzs_in", T.zqs0[:, 0:128], T.rzs[:]),
          xfer(rl[1], half[1], "rzs_in", T.zqs0[:, 128:256], T.rzs[:]))
    values(1, 1, 0)
    need(g, "zq_ok1")
    g.remote_dma(u8(T.lz[:, s]), u8(T.zq1[:, 0:128]), S["z_in%d" % rank], S.sz, pid, rid, bits(far))
    g.remote_dma(T.lzs[:, s], T.zqs1[:, 0:128], S["z_in%d" % rank], S.sz, pid, rid, bits(far))
    n["sz"] = 2 * len(chip) + 2 * len(far)

    need(V, "ld_u")
    done(V.quantize_mx(T.qu[:], T.qus[:], T.ut[:]), "qu_ok")
    done(V.tensor_copy(slot, T.run0[:, 511:513]), "m1")
    need(V, "m1", *["b_in%d" % q for q in order[1:]])
    done(V.tensor_reduce(T.mx[:], T.best[:, 0:16:4], AxisListType.X, OP.max), "m2")
    need(V, "m2")
    done(V.tensor_scalar(T.t4[:], T.best[:, 0:16:4], T.mx[:], 4096.0, OP.is_lt, OP.mult), "m3")
    need(V, "m3", "lc_in", "ln_in")
    done(V.tensor_tensor(T.c1[:], T.t4[:], T.lc[:], OP.add), "m4")
    done(V.tensor_tensor(T.c2[:], T.t4[:], T.ln[:], OP.add), "m4")
    need(V, "m4")
    done(V.tensor_reduce(T.pick[:], T.c1[:], AxisListType.X, OP.min), "pick_ok")
    done(V.tensor_tensor(T.c3[:], T.c2[:], T.best[:, 1:16:4], OP.add), "m5")
    need(V, "pick_ok", "m5")
    done(V.tensor_scalar(T.xf[:], T.mask[:], T.pick[:], 0.25, OP.mult, OP.mult), "xf_ok")
    done(V.tensor_reduce(T.won[:], T.c3[:], AxisListType.X, OP.min), "won_ok")
    need(Y, "won_ok")
    done(Y.dma_start(T.win[:], T.won[:]), "st", 16)
    need(V, "xf_ok")
    done(V.transpose(T.yf[:], T.xf[:]), "yf_ok")
    need(V, "yf_ok")
    done(V.tensor_tensor_scan(T.wf[:], T.keep[:, 0:64], T.yf[:], 0.0, OP.mult, OP.add), "wf_ok")
    need(V, "wf_ok")
    for c in range(4):
        for to in (c, c ^ 1):
            done(V.tensor_copy(T.of[32 * to:32 * to + 32, 2 * c:2 * c + 2], T.wf[32 * c:32 * c + 32, 31:64:32]), "of1_ok")
    need(V, "of1_ok")
    done(V.tensor_copy(T.of[0:64, 4:8], T.of[64:128, 4:8]), "of2_ok")
    done(V.tensor_copy(T.of[64:128, 0:4], T.of[0:64, 0:4]), "of2_ok")

    for i in range(4):
        q = order[i]
        if i == 0:
            need(P, "qu_ok", "zq_ok1")
            r, rs = T.zq1[:, 128:256], T.zqs1[:, 128:256]
        else:
            need(P, "z_in%d" % q)
            r, rs = T.lz[:, 128 * q:128 * q + 128], T.lzs[:, 128 * q:128 * q + 128]
        if i == 2:
            need(P, "ms_ok2")
        done(P.matmul_mx(T.pu[:, 512 * i:512 * i + 128], T.qu[:], T.qus[:], r, rs, True, True), "pu_ok%d" % i)
        to, frm = T.prod[:, 128 * q:128 * q + 128], T.pu[:, 512 * i:512 * i + 128]
        if i in (0, 2):
            need(V, "pu_ok%d" % i)
            done(V.tensor_copy(to, frm), "uv")
        else:
            need(A, "pu_ok%d" % i)
            done(A.activation(to, frm, ACT.Copy), "us")
    need(V, "of2_ok", "uv", "us")
    done(V.tensor_copy(T.ysb[:], T.prod[:].indirect(T.of[:, 0:8])), "y_ok")
    need(Y, "y_ok")
    done(Y.dma_start(T.y[:], T.ysb[:]), "st", 16)
    need(Y, "st")
    need(g, "sf", "sp", "sb", "sz")


def relay_program(g, core, T, topo, r, d, place):
    S = T.sem
    V = g.vector
    dst = T.cores[d]
    rid, pid = topo.addr(dst, core)
    m = topo.mask(core, dst)
    e = len(topo.engines(core, dst))
    if place:
        g.iota(T.ip[:], [[0, 4]], 0, 1).then_inc(S.k0, 1)
        g.iota(T.cp[:], [[128, 4]], 0, 1, allow_small_or_imprecise_dtypes=True).then_inc(S.k0, 1)
        V.wait_ge(S.k0, 2)
        V.tensor_scalar(T.i1[:], T.ip[:], 4, 1, OP.arith_shift_right, OP.bitwise_and).then_inc(S.k3, 1)
        V.tensor_scalar(T.i2[:], T.ip[:], 6, None, OP.arith_shift_right).then_inc(S.k3, 1)
        V.wait_ge(S.k3, 2)
        V.tensor_tensor(T.i3[:], T.i1[:], T.i2[:], OP.subtract).then_inc(S.k4, 1)
        V.wait_ge(S.k4, 1)
        V.tensor_scalar(T.cd[:], T.i3[:], 48.0, None, OP.mult).then_inc(S.k5, 1)
        V.wait_ge(S.k5, 1)
        V.tensor_tensor(T.cq[:], T.cp[:], T.cd[:], OP.add).then_inc(S.k1, 1)
        g.wait_ge(S.k1, 1)
        g.remote_dma(T.lc[:], T.cq[:], S.lc_in, S.rsent, pid, rid, m)
    else:
        g.iota(T.nq[:], [[512, 4]], 0, 0, allow_small_or_imprecise_dtypes=True).then_inc(S.k0, 1)
        g.wait_ge(S.k0, 1)
        g.remote_dma(T.ln[:], T.nq[:], S.ln_in, S.rsent, pid, rid, m)
    src = T.cores[r]
    chip = topo.engines(src, core)
    rest = [x for x in chip if x not in topo.engines(src, [c for i, c in enumerate(T.cores) if i != r and topo.may_write(src, c)][0])]
    s = slice(128 * r, 128 * r + 128)
    hops = [
        ("rf_in", 2, T.lf[:, r:r + 1], T.rfb[:], "f_in"),
        ("rac_in", len(chip) // 2, u8(T.la[:, s]), u8(T.rac[:]), "a_in"),
        ("ras_in", len(chip) // 2, T.las[:, s], T.ras[:], "a_in"),
        ("rb_in", len(rest) // 2, T.best[:, 4 * r:4 * r + 2], T.rbest[:], "b_in"),
        ("rzc_in", len(chip) // 2, u8(T.lz[:, s]), u8(T.rzc[:]), "z_in"),
        ("rzs_in", len(chip) // 2, T.lzs[:, s], T.rzs[:], "z_in"),
    ]
    for sem, k, to, frm, there in hops:
        g.wait_ge(S[sem], k)
        g.remote_dma(to, frm, S["%s%d" % (there, r)], S.rsent, pid, rid, m)
    g.wait_ge(S.rsent, (1 + len(hops)) * e)
